import numpy as np
import ml_dtypes


def mxq(x, axis, fmt="e4m3"):
    dtype, down = {"e4m3": (ml_dtypes.float8_e4m3fn, 7), "e5m2": (ml_dtypes.float8_e5m2, 14)}[fmt]
    v = np.moveaxis(np.asarray(x, np.float32).astype(ml_dtypes.bfloat16).astype(np.float64), axis, -1)
    blocks = v.reshape(v.shape[:-1] + (-1, 32))
    amax = np.abs(blocks).max(-1, keepdims=True)
    byte = np.maximum(np.where(amax > 0, np.frexp(amax)[1] - 1 + 127, 0) - down, 1)
    scale = np.exp2(byte - 127.0)
    codes = (blocks / scale).astype(np.float32).astype(dtype).astype(np.float64)
    return np.moveaxis((codes * scale).reshape(v.shape), -1, axis)


WIDE = False


def mx_kscale(k):
    if not WIDE:
        return np.ones(k)
    levels = np.array([10, -10, 5, -5, 0])
    if k % 512:
        return np.exp2(np.random.permutation(np.resize(levels, k // 32))).repeat(32)
    a = np.empty((k // 512, 16))
    for p in range(k // 512):
        a[p, :8] = np.random.permutation(np.resize(levels, 8))
        for g in range(8):
            far = levels[np.abs(levels - a[p, g]) >= 10]
            a[p, g + 8] = far[np.random.randint(len(far))]
    return np.exp2(a.ravel()).repeat(32)


def f64(x):
    return np.asarray(x).astype(np.float64)


def striped(idx):
    return np.tile(idx.reshape(-1, 16).T, (8, 1)).astype(np.uint16)


def unstriped(offs):
    return offs[:16].T.reshape(-1).astype(np.int64)


E2M1 = np.array([0.0, 0.5, 1.0, 1.5, 2.0, 3.0, 4.0, 6.0, -0.0, -0.5, -1.0, -1.5, -2.0, -3.0, -4.0, -6.0])


def pack_weight(w, fmt):
    k, n = w.shape
    w = f64(np.asarray(w, np.float32).astype(ml_dtypes.bfloat16)).reshape(k // 32, 32, n)
    amax = np.abs(w).max(1)
    if fmt == "e4m3":
        byte = np.frexp(amax)[1] - 1 + 127 - 7
    else:
        mant, ex = np.frexp(amax / 6.0)
        byte = np.where(mant > 0.5, ex, ex - 1) + 127
    byte = np.clip(np.where(amax > 0, byte, 1), 1, 254)
    scaled = (w * np.exp2(127.0 - byte)[:, None, :]).reshape(k, n).astype(np.float32)
    by_word = np.ascontiguousarray(scaled.reshape(k // 512, 128, 4, n).transpose(0, 1, 3, 2))
    if fmt == "e4m3":
        words = by_word.astype(ml_dtypes.float8_e4m3fn).view(np.uint8)
    else:
        c = by_word.astype(ml_dtypes.float4_e2m1fn).view(np.uint8) & 0xF
        words = (c[..., 0::2] | (c[..., 1::2] << 4)).reshape(k // 512, 128, 2 * n)
    return np.ascontiguousarray(words), np.ascontiguousarray(byte.astype(np.uint8).reshape(k // 512, 16, n))


def unpack_weight(words, scales, fmt):
    g, _, n = scales.shape
    words = np.ascontiguousarray(words).reshape(g, 128, n, -1)
    if fmt == "e4m3":
        vals = words.view(ml_dtypes.float8_e4m3fn).astype(np.float64)
    else:
        nib = np.empty((g, 128, n, 4), np.uint8)
        nib[..., 0::2] = words & 0xF
        nib[..., 1::2] = words >> 4
        vals = E2M1[nib]
    vals = vals * np.repeat(np.exp2(scales.astype(np.float64) - 127.0), 8, axis=1)[..., None]
    return vals.transpose(0, 1, 3, 2).reshape(g * 512, n)


def pack_table(v):
    words, scales = pack_weight(v, "e4m3")
    return np.concatenate([words.reshape(words.shape[0], -1), scales.reshape(scales.shape[0], -1)], axis=1)


def unpack_table(tab):
    g, t = tab.shape[0], tab.shape[1] // 528
    return unpack_weight(tab[:, :512 * t].reshape(g, 128, t, 4), tab[:, 512 * t:].reshape(g, 16, t), "e4m3")


K, M, T, S = 1536, 256, 1024, 512


def setup_inputs():
    n = np.random.standard_normal
    s = mx_kscale(K)[:, None]
    return {
        "tab": pack_table(n((K, T)) * s),
        "w": (n((K, M)) / np.sqrt(K) / s).astype(np.float32),
        "b": (0.3 * n(256)).astype(np.float32),
        "wgo": np.tile(np.random.uniform(0.5, 2.0, S), (128, 1)).astype(np.float32),
        "offs": striped(np.random.permutation(T)[:S]),
        "offs2": striped(np.random.permutation(T)[:S]),
    }


def reference(tab, w, b, wgo, offs, offs2):
    tab_ = unpack_table(tab)[:, unstriped(offs)]
    w_ = mxq(f64(w), 0, "e4m3")
    y = w_.T @ tab_
    out = np.zeros((M, T))
    out[:, unstriped(offs2)] = f64(wgo)[0] * (y + f64(b)[:, None])
    return out

@@ -1,0 +1,133 @@
+from contextlib import ExitStack
+
+import concourse.mybir as mybir
+
+K, M, T, S = 1536, 256, 1024, 512
+FLOPS = 2 * K * M * S
+
+F32 = mybir.dt.float32
+BF16 = mybir.dt.bfloat16
+I32 = mybir.dt.int32
+U32 = mybir.dt.uint32
+U16 = mybir.dt.uint16
+U8 = mybir.dt.uint8
+FP8X4 = mybir.dt.float8_e4m3fn_x4
+MULT = mybir.AluOpType.mult
+IDENT = mybir.ActivationFunctionType.Identity
+
+P = 128
+PASSES = K // 512
+HALVES = M // 128
+
+
+def tile_list_tabscat_bias_kernel(tc, tab, w, b, wgo, offs, offs2, out):
+    nc = tc.nc
+    with ExitStack() as ctx:
+        lists = ctx.enter_context(tc.tile_pool(name="lists", bufs=1))
+        keep = ctx.enter_context(tc.tile_pool(name="keep", bufs=1))
+        psum = ctx.enter_context(tc.psum_pool(name="psum", bufs=1))
+
+        offs_sb = lists.tile([P, S // 16], U16, name="offs_sb")
+        offs2_sb = lists.tile([P, S // 16], U16, name="offs2_sb")
+
+        scale_tab = keep.tile([P, T // 4], I32, name="scale_tab", align_bytes=64)
+        nc.vector.memset(scale_tab[:], 0)
+
+        nc.sync.dma_start(offs_sb[:], offs)
+        tab_words = [keep.tile([P, T], I32, name=f"tab_words{a}", align_bytes=64) for a in range(PASSES)]
+        w_raw = [keep.tile([P, 4, M], F32, name=f"w_raw{a}", align_bytes=64) for a in range(PASSES)]
+
+        def load_tab(a):
+            nc.sync.dma_start(tab_words[a][:], tab[a, 0 : 512 * T].rearrange("(p x) -> p x", p=P).bitcast(I32))
+
+        def load_w(a):
+            nc.sync.dma_start(w_raw[a][:], w[512 * a : 512 * (a + 1), :].rearrange("(p j) n -> p j n", j=4))
+
+        load_tab(0)
+        for q in range(4):
+            nc.scalar.dma_start(
+                scale_tab[32 * q : 32 * q + 12, :],
+                tab[:, 512 * T + 4 * T * q : 512 * T + 4 * T * (q + 1)].rearrange("a (r t) -> a r t", r=4).bitcast(I32),
+            )
+        load_w(0)
+        load_tab(1)
+        load_tab(2)
+        load_w(1)
+        nc.sync.dma_start(offs2_sb[:], offs2)
+        load_w(2)
+        wgo_sb = keep.tile([P, S], F32, name="wgo_sb")
+        nc.sync.dma_start(wgo_sb[:], wgo)
+        bias = [keep.tile([P, 1], F32, name=f"bias{h}") for h in range(HALVES)]
+        for h in range(HALVES):
+            nc.gpsimd.dma_start(bias[h][:], b[128 * h : 128 * (h + 1)].unsqueeze(1))
+
+        warm = keep.tile([P, 1], F32, name="warm")
+        nc.vector.memset(warm[:], 0.0)
+        nc.scalar.activation(warm[:], warm[:], IDENT)
+
+        placed = [keep.tile([P, T], F32, name=f"placed{h}") for h in range(HALVES)]
+        for h in range(HALVES):
+            nc.vector.memset(placed[h][:], 0.0)
+
+        words = [keep.tile([P, S], U32, name=f"words{a}", align_bytes=64) for a in range(PASSES)]
+        scales = keep.tile([P, S], U8, name="scales", align_bytes=64)
+        w_bf = [[keep.tile([P, 128, 4], BF16, name=f"w_bf{a}{h}", align_bytes=64) for h in range(HALVES)] for a in range(PASSES)]
+        w_words = [keep.tile([P, M], U32, name=f"w_words{a}", align_bytes=64) for a in range(PASSES)]
+        w_scales = [keep.tile([P, M], U8, name=f"w_scales{a}", align_bytes=64) for a in range(PASSES)]
+        acc = [psum.tile([P, S], F32, name=f"acc{h}") for h in range(HALVES)]
+
+        def gather_words(a):
+            nc.vector.tensor_copy(words[a][:], tab_words[a][:].bitcast(U32).indirect(offs_sb[:]))
+
+        def round_w(a, h, engine_copy):
+            engine_copy(
+                w_bf[a][h][:].rearrange("p (c i) j -> p c j i", i=4),
+                w_raw[a][:, :, 128 * h : 128 * (h + 1)].rearrange("p j (c i) -> p c j i", i=4),
+            )
+
+        def quantise_w(a, h):
+            cols = slice(128 * h, 128 * (h + 1))
+            nc.vector.quantize_mx(
+                w_words[a][:, cols].bitcast(FP8X4), w_scales[a][:, cols], w_bf[a][h][:].rearrange("p n j -> p (n j)")
+            )
+
+        def multiply(a, h):
+            cols = slice(128 * h, 128 * (h + 1))
+            nc.tensor.matmul_mx(
+                acc[h][:],
+                lhsT=w_words[a][:, cols].bitcast(FP8X4),
+                lhsT_scale=w_scales[a][:, cols],
+                rhs=words[a][:].bitcast(FP8X4),
+                rhs_scale=scales[4 * a : P, :],
+                start=(a == 0),
+                stop=(a == PASSES - 1),
+            )
+
+        gather_words(0)
+        nc.vector.tensor_copy(scales[:], scale_tab[:].bitcast(U8).indirect(offs_sb[:]))
+        round_w(0, 0, nc.scalar.copy)
+        round_w(0, 1, nc.scalar.copy)
+        gather_words(1)
+        gather_words(2)
+        quantise_w(0, 0)
+        quantise_w(0, 1)
+        multiply(0, 0)
+        multiply(0, 1)
+        round_w(1, 0, nc.vector.tensor_copy)
+        round_w(1, 1, nc.scalar.copy)
+        quantise_w(1, 0)
+        multiply(1, 0)
+        quantise_w(1, 1)
+        multiply(1, 1)
+        round_w(2, 0, nc.vector.tensor_copy)
+        round_w(2, 1, nc.scalar.copy)
+        quantise_w(2, 0)
+        multiply(2, 0)
+        quantise_w(2, 1)
+        multiply(2, 1)
+        y = [keep.tile([P, S], F32, name=f"y{h}") for h in range(HALVES)]
+        for h in range(HALVES):
+            nc.scalar.activation(y[h][:], acc[h][:], IDENT, bias=bias[h][:])
+        for h in range(HALVES):
+            nc.vector.tensor_tensor(placed[h][:].indirect(offs2_sb[:]), y[h][:], wgo_sb[:], MULT)
+            nc.sync.dma_start(out[128 * h : 128 * (h + 1), :], placed[h][:])

@@ -18,6 +18,8 @@ IDENT = mybir.ActivationFunctionType.Identity
 P = 128
 PASSES = K // 512
 HALVES = M // 128
+PIECES = 2
+PIECE = S // PIECES
 
 
 def tile_list_tabscat_bias_kernel(tc, tab, w, b, wgo, offs, offs2, out):
@@ -43,23 +45,28 @@ def tile_list_tabscat_bias_kernel(tc, tab, w, b, wgo, offs, offs2, out):
         def load_w(a):
             nc.sync.dma_start(w_raw[a][:], w[512 * a : 512 * (a + 1), :].rearrange("(p j) n -> p j n", j=4))
 
-        load_tab(0)
-        for q in range(4):
-            nc.scalar.dma_start(
+        def load_scales(queue, q):
+            queue.dma_start(
                 scale_tab[32 * q : 32 * q + 12, :],
                 tab[:, 512 * T + 4 * T * q : 512 * T + 4 * T * (q + 1)].rearrange("a (r t) -> a r t", r=4).bitcast(I32),
             )
-        load_w(0)
-        load_tab(1)
-        load_tab(2)
-        load_w(1)
-        nc.sync.dma_start(offs2_sb[:], offs2)
-        load_w(2)
-        wgo_sb = keep.tile([P, S], F32, name="wgo_sb")
-        nc.sync.dma_start(wgo_sb[:], wgo)
+
+        load_tab(0)
         bias = [keep.tile([P, 1], F32, name=f"bias{h}") for h in range(HALVES)]
         for h in range(HALVES):
             nc.gpsimd.dma_start(bias[h][:], b[128 * h : 128 * (h + 1)].unsqueeze(1))
+        load_scales(nc.scalar, 0)
+        load_scales(nc.scalar, 1)
+        load_w(0)
+        load_scales(nc.sync, 2)
+        load_scales(nc.sync, 3)
+        load_tab(1)
+        load_w(1)
+        load_w(2)
+        load_tab(2)
+        nc.sync.dma_start(offs2_sb[:], offs2)
+        wgo_sb = keep.tile([P, S], F32, name="wgo_sb")
+        nc.sync.dma_start(wgo_sb[:], wgo)
 
         warm = keep.tile([P, 1], F32, name="warm")
         nc.vector.memset(warm[:], 0.0)
@@ -71,63 +78,65 @@ def tile_list_tabscat_bias_kernel(tc, tab, w, b, wgo, offs, offs2, out):
 
         words = [keep.tile([P, S], U32, name=f"words{a}", align_bytes=64) for a in range(PASSES)]
         scales = keep.tile([P, S], U8, name="scales", align_bytes=64)
-        w_bf = [[keep.tile([P, 128, 4], BF16, name=f"w_bf{a}{h}", align_bytes=64) for h in range(HALVES)] for a in range(PASSES)]
+        w_bf = [keep.tile([P, M, 4], BF16, name=f"w_bf{a}", align_bytes=64) for a in range(2)]
+        w_bf_last = [keep.tile([P, 128, 4], BF16, name=f"w_bf_last{h}", align_bytes=64) for h in range(HALVES)]
         w_words = [keep.tile([P, M], U32, name=f"w_words{a}", align_bytes=64) for a in range(PASSES)]
         w_scales = [keep.tile([P, M], U8, name=f"w_scales{a}", align_bytes=64) for a in range(PASSES)]
-        acc = [psum.tile([P, S], F32, name=f"acc{h}") for h in range(HALVES)]
+        acc0 = [psum.tile([P, PIECE], F32, name=f"acc0{c}") for c in range(PIECES)]
+        acc1 = psum.tile([P, S], F32, name="acc1")
+        y0 = [keep.tile([P, PIECE], F32, name=f"y0{c}") for c in range(PIECES)]
+        y1 = keep.tile([P, S], F32, name="y1")
 
-        def gather_words(a):
-            nc.vector.tensor_copy(words[a][:], tab_words[a][:].bitcast(U32).indirect(offs_sb[:]))
+        def gather_words(a, first=0, end=S):
+            nc.vector.tensor_copy(words[a][:, first:end], tab_words[a][:].bitcast(U32).indirect(offs_sb[:, first // 16 : end // 16]))
 
-        def round_w(a, h, engine_copy):
-            engine_copy(
-                w_bf[a][h][:].rearrange("p (c i) j -> p c j i", i=4),
-                w_raw[a][:, :, 128 * h : 128 * (h + 1)].rearrange("p j (c i) -> p c j i", i=4),
+        def quantise_w(a, cols, rounded):
+            nc.scalar.copy(
+                rounded.rearrange("p (c i) j -> p c j i", i=4),
+                w_raw[a][:, :, cols].rearrange("p j (c i) -> p c j i", i=4),
             )
+            nc.vector.quantize_mx(w_words[a][:, cols].bitcast(FP8X4), w_scales[a][:, cols], rounded.rearrange("p n j -> p (n j)"))
 
-        def quantise_w(a, h):
-            cols = slice(128 * h, 128 * (h + 1))
-            nc.vector.quantize_mx(
-                w_words[a][:, cols].bitcast(FP8X4), w_scales[a][:, cols], w_bf[a][h][:].rearrange("p n j -> p (n j)")
-            )
-
-        def multiply(a, h):
-            cols = slice(128 * h, 128 * (h + 1))
+        def multiply(acc, a, h, cols):
+            rows = slice(128 * h, 128 * (h + 1))
             nc.tensor.matmul_mx(
-                acc[h][:],
-                lhsT=w_words[a][:, cols].bitcast(FP8X4),
-                lhsT_scale=w_scales[a][:, cols],
-                rhs=words[a][:].bitcast(FP8X4),
-                rhs_scale=scales[4 * a : P, :],
+                acc[:],
+                lhsT=w_words[a][:, rows].bitcast(FP8X4),
+                lhsT_scale=w_scales[a][:, rows],
+                rhs=words[a][:, cols].bitcast(FP8X4),
+                rhs_scale=scales[4 * a : P, cols],
                 start=(a == 0),
                 stop=(a == PASSES - 1),
             )
 
+        def scatter(h, values, first, count):
+            nc.vector.tensor_tensor(
+                placed[h][:].indirect(offs2_sb[:, first // 16 : (first + count) // 16]),
+                values,
+                wgo_sb[:, first : first + count],
+                MULT,
+            )
+
+        pieces = [slice(PIECE * c, PIECE * (c + 1)) for c in range(PIECES)]
         gather_words(0)
         nc.vector.tensor_copy(scales[:], scale_tab[:].bitcast(U8).indirect(offs_sb[:]))
-        round_w(0, 0, nc.scalar.copy)
-        round_w(0, 1, nc.scalar.copy)
         gather_words(1)
-        gather_words(2)
-        quantise_w(0, 0)
-        quantise_w(0, 1)
-        multiply(0, 0)
-        multiply(0, 1)
-        round_w(1, 0, nc.vector.tensor_copy)
-        round_w(1, 1, nc.scalar.copy)
-        quantise_w(1, 0)
-        multiply(1, 0)
-        quantise_w(1, 1)
-        multiply(1, 1)
-        round_w(2, 0, nc.vector.tensor_copy)
-        round_w(2, 1, nc.scalar.copy)
-        quantise_w(2, 0)
-        multiply(2, 0)
-        quantise_w(2, 1)
-        multiply(2, 1)
-        y = [keep.tile([P, S], F32, name=f"y{h}") for h in range(HALVES)]
+        for a in range(2):
+            quantise_w(a, slice(0, M), w_bf[a][:])
         for h in range(HALVES):
-            nc.scalar.activation(y[h][:], acc[h][:], IDENT, bias=bias[h][:])
-        for h in range(HALVES):
-            nc.vector.tensor_tensor(placed[h][:].indirect(offs2_sb[:]), y[h][:], wgo_sb[:], MULT)
-            nc.sync.dma_start(out[128 * h : 128 * (h + 1), :], placed[h][:])
+            quantise_w(2, slice(128 * h, 128 * (h + 1)), w_bf_last[h][:])
+        for a in range(2):
+            for c in range(PIECES):
+                multiply(acc0[c], a, 0, pieces[c])
+        for c in range(PIECES):
+            gather_words(2, PIECE * c, PIECE * (c + 1))
+            multiply(acc0[c], 2, 0, pieces[c])
+            nc.scalar.activation(y0[c][:], acc0[c][:], IDENT, bias=bias[0][:])
+        for a in range(PASSES):
+            multiply(acc1, a, 1, slice(0, S))
+        nc.scalar.activation(y1[:], acc1[:], IDENT, bias=bias[1][:])
+        for c in range(PIECES):
+            scatter(0, y0[c][:], PIECE * c, PIECE)
+        nc.sync.dma_start(out[0:P, :], placed[0][:])
+        scatter(1, y1[:], 0, S)
+        nc.sync.dma_start(out[P : 2 * P, :], placed[1][:])

from contextlib import ExitStack

import concourse.mybir as mybir

K, M, T, S = 1536, 256, 1024, 512
FLOPS = 2 * K * M * S

F32 = mybir.dt.float32
BF16 = mybir.dt.bfloat16
I32 = mybir.dt.int32
U32 = mybir.dt.uint32
U16 = mybir.dt.uint16
U8 = mybir.dt.uint8
FP8X4 = mybir.dt.float8_e4m3fn_x4
MULT = mybir.AluOpType.mult
IDENT = mybir.ActivationFunctionType.Identity

P = 128
PASSES = K // 512
HALVES = M // 128
PIECES = 2
PIECE = S // PIECES


def tile_list_tabscat_bias_kernel(tc, tab, w, b, wgo, offs, offs2, out):
    nc = tc.nc
    with ExitStack() as ctx:
        lists = ctx.enter_context(tc.tile_pool(name="lists", bufs=1))
        keep = ctx.enter_context(tc.tile_pool(name="keep", bufs=1))
        psum = ctx.enter_context(tc.psum_pool(name="psum", bufs=1))

        offs_sb = lists.tile([P, S // 16], U16, name="offs_sb")
        offs2_sb = lists.tile([P, S // 16], U16, name="offs2_sb")

        scale_tab = keep.tile([P, T // 4], I32, name="scale_tab", align_bytes=64)
        nc.vector.memset(scale_tab[:], 0)

        nc.sync.dma_start(offs_sb[:], offs)
        tab_words = [keep.tile([P, T], I32, name=f"tab_words{a}", align_bytes=64) for a in range(PASSES)]
        w_raw = [keep.tile([P, 4, M], F32, name=f"w_raw{a}", align_bytes=64) for a in range(PASSES)]

        def load_tab(a):
            nc.sync.dma_start(tab_words[a][:], tab[a, 0 : 512 * T].rearrange("(p x) -> p x", p=P).bitcast(I32))

        def load_w(a):
            nc.sync.dma_start(w_raw[a][:], w[512 * a : 512 * (a + 1), :].rearrange("(p j) n -> p j n", j=4))

        def load_scales(queue, q):
            queue.dma_start(
                scale_tab[32 * q : 32 * q + 12, :],
                tab[:, 512 * T + 4 * T * q : 512 * T + 4 * T * (q + 1)].rearrange("a (r t) -> a r t", r=4).bitcast(I32),
            )

        load_tab(0)
        bias = [keep.tile([P, 1], F32, name=f"bias{h}") for h in range(HALVES)]
        for h in range(HALVES):
            nc.gpsimd.dma_start(bias[h][:], b[128 * h : 128 * (h + 1)].unsqueeze(1))
        load_scales(nc.scalar, 0)
        load_scales(nc.scalar, 1)
        load_w(0)
        load_scales(nc.sync, 2)
        load_scales(nc.sync, 3)
        load_tab(1)
        load_w(1)
        load_w(2)
        load_tab(2)
        nc.sync.dma_start(offs2_sb[:], offs2)
        wgo_sb = keep.tile([P, S], F32, name="wgo_sb")
        nc.sync.dma_start(wgo_sb[:], wgo)

        warm = keep.tile([P, 1], F32, name="warm")
        nc.vector.memset(warm[:], 0.0)
        nc.scalar.activation(warm[:], warm[:], IDENT)

        placed = [keep.tile([P, T], F32, name=f"placed{h}") for h in range(HALVES)]
        for h in range(HALVES):
            nc.vector.memset(placed[h][:], 0.0)

        words = [keep.tile([P, S], U32, name=f"words{a}", align_bytes=64) for a in range(PASSES)]
        scales = keep.tile([P, S], U8, name="scales", align_bytes=64)
        w_bf = [keep.tile([P, M, 4], BF16, name=f"w_bf{a}", align_bytes=64) for a in range(2)]
        w_bf_last = [keep.tile([P, 128, 4], BF16, name=f"w_bf_last{h}", align_bytes=64) for h in range(HALVES)]
        w_words = [keep.tile([P, M], U32, name=f"w_words{a}", align_bytes=64) for a in range(PASSES)]
        w_scales = [keep.tile([P, M], U8, name=f"w_scales{a}", align_bytes=64) for a in range(PASSES)]
        acc0 = [psum.tile([P, PIECE], F32, name=f"acc0{c}") for c in range(PIECES)]
        acc1 = psum.tile([P, S], F32, name="acc1")
        y0 = [keep.tile([P, PIECE], F32, name=f"y0{c}") for c in range(PIECES)]
        y1 = keep.tile([P, S], F32, name="y1")

        def gather_words(a, first=0, end=S):
            nc.vector.tensor_copy(words[a][:, first:end], tab_words[a][:].bitcast(U32).indirect(offs_sb[:, first // 16 : end // 16]))

        def quantise_w(a, cols, rounded):
            nc.scalar.copy(
                rounded.rearrange("p (c i) j -> p c j i", i=4),
                w_raw[a][:, :, cols].rearrange("p j (c i) -> p c j i", i=4),
            )
            nc.vector.quantize_mx(w_words[a][:, cols].bitcast(FP8X4), w_scales[a][:, cols], rounded.rearrange("p n j -> p (n j)"))

        def multiply(acc, a, h, cols):
            rows = slice(128 * h, 128 * (h + 1))
            nc.tensor.matmul_mx(
                acc[:],
                lhsT=w_words[a][:, rows].bitcast(FP8X4),
                lhsT_scale=w_scales[a][:, rows],
                rhs=words[a][:, cols].bitcast(FP8X4),
                rhs_scale=scales[4 * a : P, cols],
                start=(a == 0),
                stop=(a == PASSES - 1),
            )

        def scatter(h, values, first, count):
            nc.vector.tensor_tensor(
                placed[h][:].indirect(offs2_sb[:, first // 16 : (first + count) // 16]),
                values,
                wgo_sb[:, first : first + count],
                MULT,
            )

        pieces = [slice(PIECE * c, PIECE * (c + 1)) for c in range(PIECES)]
        gather_words(0)
        nc.vector.tensor_copy(scales[:], scale_tab[:].bitcast(U8).indirect(offs_sb[:]))
        gather_words(1)
        for a in range(2):
            quantise_w(a, slice(0, M), w_bf[a][:])
        for h in range(HALVES):
            quantise_w(2, slice(128 * h, 128 * (h + 1)), w_bf_last[h][:])
        for a in range(2):
            for c in range(PIECES):
                multiply(acc0[c], a, 0, pieces[c])
        for c in range(PIECES):
            gather_words(2, PIECE * c, PIECE * (c + 1))
            multiply(acc0[c], 2, 0, pieces[c])
            nc.scalar.activation(y0[c][:], acc0[c][:], IDENT, bias=bias[0][:])
        for a in range(PASSES):
            multiply(acc1, a, 1, slice(0, S))
        nc.scalar.activation(y1[:], acc1[:], IDENT, bias=bias[1][:])
        for c in range(PIECES):
            scatter(0, y0[c][:], PIECE * c, PIECE)
        nc.sync.dma_start(out[0:P, :], placed[0][:])
        scatter(1, y1[:], 0, S)
        nc.sync.dma_start(out[P : 2 * P, :], placed[1][:])
